import numpy as np, ml_dtypes
CORES = [36,38,116,118,124,126,164,166,244,246,252,254]
N = 12
TK = 32
def setup_inputs(rng):
    x = rng.standard_normal((N, 128, TK), dtype=np.float32).astype(ml_dtypes.bfloat16); w1 = (rng.standard_normal((N, 128, 128), dtype=np.float32) / 8).astype(ml_dtypes.bfloat16)
    wa = np.concatenate(list(w1.astype(np.float64)), axis=1)
    for r in range(N):
        while True:
            near = (np.abs(wa.T @ x[r].astype(np.float64)) < 2e-4).any(axis=0)
            if not near.any(): break
            x[r][:, near] = rng.standard_normal((128, int(near.sum())), dtype=np.float32).astype(ml_dtypes.bfloat16)
    return {"x": x, "dy": rng.standard_normal((N, 128, TK), dtype=np.float32).astype(ml_dtypes.bfloat16), "w1": w1, "w2t": (rng.standard_normal((N, 128, 128), dtype=np.float32) / 8).astype(ml_dtypes.bfloat16)}
def setup_inputs_big(rng):
    d = setup_inputs(rng)
    for k in ("x", "dy", "w1", "w2t"): d[k] = (d[k].astype(np.float32) * 1024.0).astype(d[k].dtype)
    return d
def setup_inputs_small(rng):
    d = setup_inputs(rng)
    for k in ("x", "dy", "w1", "w2t"): d[k] = (d[k].astype(np.float32) * (1 / 1024.0)).astype(d[k].dtype)
    return d
def setup_inputs_apart(rng):
    d = setup_inputs(rng)
    f = (10.0 ** rng.permutation(np.linspace(-1.5, 1.5, N))).astype(np.float32).reshape(N, 1, 1)
    for k in ("x", "dy", "w1", "w2t"): d[k] = (d[k].astype(np.float32) * f).astype(d[k].dtype)
    return d
def reference(x, dy, w1, w2t):
    X, DY, W1, W2T = x.astype(np.float64), dy.astype(np.float64), w1.astype(np.float64), w2t.astype(np.float64)
    dx = np.zeros((N, 128, TK))
    for r in range(N):
        for j in range(N):
            dx[r] += W1[j] @ ((W1[j].T @ X[r] > 0) * (W2T[j].T @ DY[r]))
    return {"dx": dx.astype(ml_dtypes.bfloat16)}

@@ -1,0 +1,214 @@
+from concourse.bass import DstId, RemoteDMATransfer
+from concourse.mybir import AluOpType, ActivationFunctionType
+
+TK = 32
+BL = 2 * TK
+PR = 2 * BL
+MAXG = 4
+
+SCRATCH = {
+    "X": ("sbuf", [128, PR * (1 + MAXG)], "bfloat16"),
+    "WB": ("sbuf", [128, 512], "bfloat16"),
+    "W1T": ("sbuf", [128, 256], "bfloat16"),
+    "ONES": ("sbuf", [128, 128], "bfloat16"),
+    "IDN": ("sbuf", [128, 128], "bfloat16"),
+    "M": ("sbuf", [128, PR * (1 + MAXG)], "bfloat16"),
+    "G": ("sbuf", [128, PR * (1 + MAXG)], "bfloat16"),
+    "PO": ("sbuf", [128, BL * MAXG], "bfloat16"),
+    "R": ("sbuf", [128, TK * 6], "bfloat16"),
+    "OUT": ("sbuf", [128, TK], "bfloat16"),
+    "PA": ("psum", [128, 512], "float32"),
+    "PB": ("psum", [128, 512], "float32"),
+    "PP": ("psum", [128, 512], "float32"),
+    "PF": ("psum", [128, 512], "float32"),
+    "PT0": ("psum", [128, 1024], "bfloat16"),
+    "PT1": ("psum", [128, 1024], "bfloat16"),
+}
+SEMAPHORES = (["ld_x", "ld_w", "ones", "idn", "sent", "sibx", "wsib", "tp0", "tp1", "tc0", "tc1",
+               "sa", "sb", "vm", "ga", "gb", "pp", "pc", "fin", "oc", "st"]
+              + ["xc%d" % i for i in range(6)] + ["r%d" % i for i in range(1, 6)])
+
+
+def _bits(mask):
+    return [i for i in range(16) if (mask >> i) & 1]
+
+
+def _mk(bits):
+    m = 0
+    for b in bits:
+        m |= 1 << b
+    return m
+
+
+def _plan(T, topo):
+    cores = list(T.cores)
+    keys, mem = [], {}
+    for c in cores:
+        k = (topo.host(c), topo.chip(c))
+        if k not in mem:
+            keys.append(k)
+            mem[k] = []
+        mem[k].append(c)
+    n = len(keys)
+    lo, port = [], []
+    for k in keys:
+        m = mem[k]
+        owners = [c for c in m if all(topo.may_write(c, o) for o in cores if o != c)]
+        p = owners[-1]
+        port.append(p)
+        lo.append([c for c in m if c != p][0])
+    same, cross = [], []
+    for i in range(n):
+        peers = sorted([j for j in range(n) if j != i], key=lambda j: (j - i) % n)
+        same.append([j for j in peers if topo.may_write(lo[i], lo[j])])
+        cross.append([j for j in peers if not topo.may_write(lo[i], lo[j])])
+    served = []
+    for j in range(n):
+        a = sorted([i for i in range(n) if j in same[i]], key=lambda i: (same[i].index(j), i))
+        b = sorted([i for i in range(n) if j in cross[i]], key=lambda i: (cross[i].index(j), i))
+        served.append((a, b))
+    return {"n": n, "lo": lo, "port": port, "same": same, "cross": cross, "served": served,
+            "chip_of": {c: keys.index((topo.host(c), topo.chip(c))) for c in cores}}
+
+
+def rank_program(g, core, T, topo):
+    if T.rank_of(core) is None:
+        return
+    P = _plan(T, topo)
+    S = T.sem
+    ci = P["chip_of"][core]
+    lo, port, same, cross = P["lo"], P["port"], P["same"], P["cross"]
+    is_lo = core == lo[ci]
+    sib = port[ci] if is_lo else lo[ci]
+    mine = P["served"][ci][0 if is_lo else 1]
+    X, WB, W1T, M, G, PO, R = T.X, T.WB, T.W1T, T.M, T.G, T.PO, T.R
+    pe, ve, se, sy = g.tensor, g.vector, g.scalar, g.sync
+
+    def did(d):
+        rid, pid = topo.addr(d, core)
+        return DstId(rid=rid, pnc=pid)
+
+    def slot(j, i):
+        a, b = P["served"][j]
+        return PR * (1 + (a.index(i) if i in a else b.index(i)))
+
+    rorder = same[ci] + cross[ci]
+    off = topo.mask(core, lo[same[ci][0]])
+    hi = topo.mask(core, sib) & ~off
+    n_off, n_hi = len(_bits(off)), len(_bits(hi))
+    ob = 0 if is_lo else BL
+    xc, dc = (TK, 0) if is_lo else (BL, BL + TK)
+    wc = 0 if is_lo else 256
+    sent = 0
+
+    sy.dma_start(X[:, xc:xc + TK], T.x[:]).then_inc(S.ld_x, 16)
+    se.dma_start(X[:, dc:dc + TK], T.dy[:]).then_inc(S.ld_x, 16)
+    sy.dma_start(WB[:, wc:wc + 128], T.w1[:]).then_inc(S.ld_w, 16)
+    se.dma_start(WB[:, wc + 128:wc + 256], T.w2t[:]).then_inc(S.ld_w, 16)
+    ve.memset(T.ONES[:], 1.0).then_inc(S.ones, 1)
+    g.wait_ge(S.ones, 1)
+    g.affine_select(T.IDN[:], T.ONES[:], [[-1, 128]], AluOpType.is_equal, 0.0, 0, 1).then_inc(S.idn, 1)
+
+    g.wait_ge(S.ld_x, 32)
+    own = X[:, ob:ob + BL]
+    tr = []
+    if is_lo:
+        tr.append(RemoteDMATransfer(dst_ids=[did(sib)], dma_engine_mask=hi, remote_sem=S.sibx,
+                                    srcs=[own], dsts=[X[:, 0:BL]]))
+        sent += n_hi
+    tr.append(RemoteDMATransfer(dst_ids=[did(lo[j]) for j in same[ci]], dma_engine_mask=off,
+                                remote_sem=S["xc%d" % ci], srcs=[own],
+                                dsts=[X[:, slot(j, ci) + ob:slot(j, ci) + ob + BL] for j in same[ci]]))
+    sent += n_off
+    g.remote_dma_fused(tr, local_sem=S.sent)
+
+    g.wait_ge(S.ld_w, 32)
+    rid, pid = topo.addr(sib, core)
+    g.remote_dma(WB[:, wc:wc + 256], WB[:, wc:wc + 256], S.wsib, S.sent, pid, rid, hi)
+    sent += n_hi
+
+    if not is_lo:
+        g.wait_ge(S.sibx, n_hi)
+        g.remote_dma_fused([RemoteDMATransfer(dst_ids=[did(port[j]) for j in cross[ci]], dma_engine_mask=off,
+                                              remote_sem=S["xc%d" % ci], srcs=[X[:, 0:PR]],
+                                              dsts=[X[:, slot(j, ci):slot(j, ci) + PR] for j in cross[ci]])],
+                           local_sem=S.sent)
+        sent += n_off
+
+    sc = 256 - wc
+    pe.wait_ge(S.idn, 1)
+    pe.wait_ge(S.ld_w, 32)
+    pe.transpose(T.PT0[:, 0:128], WB[:, wc:wc + 128], T.IDN[:]).then_inc(S.tp0, 1)
+    pe.wait_ge(S.wsib, n_hi)
+    pe.transpose(T.PT1[:, 0:128], WB[:, sc:sc + 128], T.IDN[:]).then_inc(S.tp1, 1)
+    se.wait_ge(S.tp0, 1)
+    se.activation(W1T[:, wc // 2:wc // 2 + 128], T.PT0[:, 0:128], ActivationFunctionType.Copy).then_inc(S.tc0, 1)
+    se.wait_ge(S.tp1, 1)
+    se.activation(W1T[:, sc // 2:sc // 2 + 128], T.PT1[:, 0:128], ActivationFunctionType.Copy).then_inc(S.tc1, 1)
+
+    cnt = {"sa": 0, "sb": 0, "vm": 0}
+    halves = (_mk(_bits(off)[:n_off // 2]), _mk(_bits(off)[n_off // 2:]))
+    for k in range(1 + len(mine)):
+        if k == 0:
+            n = TK
+            xs = [(xc, TK)]
+            ds = [dc]
+            pe.wait_ge(S.ld_x, 32)
+        else:
+            i = mine[k - 1]
+            b = PR * k
+            n = BL
+            xs = [(b + TK, BL)]
+            ds = [b, b + BL + TK]
+            pe.wait_ge(S["xc%d" % i], 2 * n_off if is_lo else n_off)
+        for sh, (bank, sem) in enumerate(((T.PA, "sa"), (T.PB, "sb"))):
+            w = 256 * sh
+            pe.matmul(bank[:, 0:n], WB[:, w:w + 128], X[:, xs[0][0]:xs[0][0] + xs[0][1]], True, True).then_inc(S[sem], 1)
+            cnt[sem] += 1
+            for q, d in enumerate(ds):
+                pe.matmul(bank[:, n + TK * q:n + TK * (q + 1)], WB[:, w + 128:w + 256], X[:, d:d + TK],
+                          True, True).then_inc(S[sem], 1)
+                cnt[sem] += 1
+        for sh, (bank, sem, gs) in enumerate(((T.PA, "sa", S.ga), (T.PB, "sb", S.gb))):
+            c = PR * k + BL * sh
+            ve.wait_ge(S[sem], cnt[sem])
+            ve.tensor_scalar(M[:, c:c + n], bank[:, 0:n], 0.0, None, AluOpType.is_gt).then_inc(S.vm, 1)
+            cnt["vm"] += 1
+            ve.wait_ge(S.vm, cnt["vm"])
+            ve.tensor_tensor(G[:, c:c + n], M[:, c:c + n], bank[:, n:2 * n], AluOpType.mult).then_inc(gs, 1)
+        if k == 0:
+            pe.wait_ge(S.tc0, 1)
+            pe.wait_ge(S.tc1, 1)
+        else:
+            pe.wait_ge(S.pc, k)
+        pe.wait_ge(S.ga, k + 1)
+        pe.matmul(T.PP[:, 0:n], W1T[:, 0:128], G[:, PR * k:PR * k + n], True, False)
+        pe.wait_ge(S.gb, k + 1)
+        pe.matmul(T.PP[:, 0:n], W1T[:, 128:256], G[:, PR * k + BL:PR * k + BL + n], False, True).then_inc(S.pp, 1)
+        ve.wait_ge(S.pp, k + 1)
+        if k == 0:
+            ve.tensor_copy(R[:, 0:TK], T.PP[:, 0:n]).then_inc(S.pc, 1)
+            continue
+        po = BL * (k - 1)
+        ve.tensor_copy(PO[:, po:po + BL], T.PP[:, 0:n]).then_inc(S.pc, 1)
+        i = mine[k - 1]
+        rs = 1 + (same[i] + cross[i]).index(ci)
+        g.wait_ge(S.pc, k + 1)
+        g.remote_dma_fused([RemoteDMATransfer(dst_ids=[did(d)], dma_engine_mask=halves[t], remote_sem=S["r%d" % rs],
+                                              srcs=[PO[:, po + TK * t:po + TK * (t + 1)]],
+                                              dsts=[R[:, TK * rs:TK * (rs + 1)]])
+                            for t, d in enumerate((lo[i], port[i]))], local_sem=S.sent)
+        sent += n_off
+
+    pe.wait_ge(S.pc, 1 + len(mine))
+    pe.matmul(T.PF[:, 0:TK], T.IDN[:], R[:, 0:TK], True, False)
+    for q in range(1, 1 + len(rorder)):
+        pe.wait_ge(S["r%d" % q], n_off // 2)
+        mm = pe.matmul(T.PF[:, 0:TK], T.IDN[:], R[:, TK * q:TK * (q + 1)], False, q == len(rorder))
+    mm.then_inc(S.fin, 1)
+    ve.wait_ge(S.fin, 1)
+    ve.tensor_copy(T.OUT[:], T.PF[:, 0:TK]).then_inc(S.oc, 1)
+    sy.wait_ge(S.oc, 1)
+    sy.dma_start(T.dx[:], T.OUT[:]).then_inc(S.st, 16)
+    sy.wait_ge(S.st, 16)
+    g.wait_ge(S.sent, sent)

@@ -1,10 +1,12 @@
 from concourse.bass import DstId, RemoteDMATransfer
 from concourse.mybir import AluOpType, ActivationFunctionType
 
+NSIM = 256
 TK = 32
 BL = 2 * TK
 PR = 2 * BL
-MAXG = 4
+MAXG = 3
+KEEP = 2
 
 SCRATCH = {
     "X": ("sbuf", [128, PR * (1 + MAXG)], "bfloat16"),
@@ -14,7 +16,7 @@ SCRATCH = {
     "IDN": ("sbuf", [128, 128], "bfloat16"),
     "M": ("sbuf", [128, PR * (1 + MAXG)], "bfloat16"),
     "G": ("sbuf", [128, PR * (1 + MAXG)], "bfloat16"),
-    "PO": ("sbuf", [128, BL * MAXG], "bfloat16"),
+    "PO": ("sbuf", [128, BL * (1 + MAXG)], "bfloat16"),
     "R": ("sbuf", [128, TK * 6], "bfloat16"),
     "OUT": ("sbuf", [128, TK], "bfloat16"),
     "PA": ("psum", [128, 512], "float32"),
@@ -50,37 +52,55 @@ def _plan(T, topo):
             mem[k] = []
         mem[k].append(c)
     n = len(keys)
+
+    def owner(c):
+        return all(topo.may_write(c, o) for o in cores if o != c)
+
     lo, port = [], []
     for k in keys:
-        m = mem[k]
-        owners = [c for c in m if all(topo.may_write(c, o) for o in cores if o != c)]
-        p = owners[-1]
+        p = [c for c in mem[k] if owner(c)][-1]
         port.append(p)
-        lo.append([c for c in m if c != p][0])
-    same, cross = [], []
+        lo.append([c for c in mem[k] if c != p][0])
+    same, cross, helpers = [], [], []
     for i in range(n):
         peers = sorted([j for j in range(n) if j != i], key=lambda j: (j - i) % n)
         same.append([j for j in peers if topo.may_write(lo[i], lo[j])])
         cross.append([j for j in peers if not topo.may_write(lo[i], lo[j])])
-    served = []
-    for j in range(n):
-        a = sorted([i for i in range(n) if j in same[i]], key=lambda i: (same[i].index(j), i))
-        b = sorted([i for i in range(n) if j in cross[i]], key=lambda i: (cross[i].index(j), i))
-        served.append((a, b))
-    return {"n": n, "lo": lo, "port": port, "same": same, "cross": cross, "served": served,
-            "chip_of": {c: keys.index((topo.host(c), topo.chip(c))) for c in cores}}
+        idle = [c for c in range(NSIM) if (topo.host(c), topo.chip(c)) == keys[i] and c not in cores and owner(c)]
+        idle.sort(key=lambda c: (topo.die(c) != topo.die(port[i]), c))
+        helpers.append(idle[:max(0, len(cross[i]) - KEEP)])
+    rel = {}
+    for i in range(n):
+        for q, j in enumerate(cross[i]):
+            rel[(i, j)] = port[i] if q < KEEP or q - KEEP >= len(helpers[i]) else helpers[i][q - KEEP]
+    role, sendl, groups = {}, {}, {}
+    for i in range(n):
+        role[lo[i]] = (i, "lo")
+        role[port[i]] = (i, "port")
+        for h in helpers[i]:
+            role[h] = (i, "helper")
+    for c, (i, kind) in role.items():
+        sendl[c] = sorted([j for j in cross[i] if rel[(i, j)] == c], key=lambda j: rel[(j, i)] != port[j])
+    for c, (j, kind) in role.items():
+        if kind == "lo":
+            groups[c] = sorted([i for i in range(n) if j in same[i]], key=lambda i: (same[i].index(j), i))
+        else:
+            groups[c] = sorted([i for i in cross[j] if rel[(j, i)] == c],
+                               key=lambda i: (rel[(i, j)] != port[i], sendl[rel[(i, j)]].index(j), i))
+    return {"lo": lo, "port": port, "same": same, "cross": cross, "helpers": helpers, "rel": rel, "role": role,
+            "sendl": sendl, "groups": groups}
 
 
 def rank_program(g, core, T, topo):
-    if T.rank_of(core) is None:
-        return
     P = _plan(T, topo)
+    if core not in P["role"]:
+        return
     S = T.sem
-    ci = P["chip_of"][core]
-    lo, port, same, cross = P["lo"], P["port"], P["same"], P["cross"]
-    is_lo = core == lo[ci]
-    sib = port[ci] if is_lo else lo[ci]
-    mine = P["served"][ci][0 if is_lo else 1]
+    ci, kind = P["role"][core]
+    lo, port, same, cross, rel = P["lo"], P["port"], P["same"], P["cross"], P["rel"]
+    hs = P["helpers"][ci]
+    mine = P["groups"][core]
+    is_lo, is_rank = kind == "lo", kind != "helper"
     X, WB, W1T, M, G, PO, R = T.X, T.WB, T.W1T, T.M, T.G, T.PO, T.R
     pe, ve, se, sy = g.tensor, g.vector, g.scalar, g.sync
 
@@ -88,82 +108,89 @@ def rank_program(g, core, T, topo):
         rid, pid = topo.addr(d, core)
         return DstId(rid=rid, pnc=pid)
 
-    def slot(j, i):
-        a, b = P["served"][j]
-        return PR * (1 + (a.index(i) if i in a else b.index(i)))
+    def slot(w, i):
+        return PR * (1 + P["groups"][w].index(i))
 
-    rorder = same[ci] + cross[ci]
-    off = topo.mask(core, lo[same[ci][0]])
-    hi = topo.mask(core, sib) & ~off
-    n_off, n_hi = len(_bits(off)), len(_bits(hi))
-    ob = 0 if is_lo else BL
-    xc, dc = (TK, 0) if is_lo else (BL, BL + TK)
-    wc = 0 if is_lo else 256
+    far = lo[same[ci][0]] if is_rank else port[P["sendl"][core][0]]
+    off = topo.mask(core, far)
+    full = topo.mask(lo[ci], port[ci])
+    hi = full & ~off
+    wm = full if hs else hi
+    n_off, n_hi, n_wm = len(_bits(off)), len(_bits(hi)), len(_bits(wm))
     sent = 0
 
-    sy.dma_start(X[:, xc:xc + TK], T.x[:]).then_inc(S.ld_x, 16)
-    se.dma_start(X[:, dc:dc + TK], T.dy[:]).then_inc(S.ld_x, 16)
-    sy.dma_start(WB[:, wc:wc + 128], T.w1[:]).then_inc(S.ld_w, 16)
-    se.dma_start(WB[:, wc + 128:wc + 256], T.w2t[:]).then_inc(S.ld_w, 16)
     ve.memset(T.ONES[:], 1.0).then_inc(S.ones, 1)
     g.wait_ge(S.ones, 1)
     g.affine_select(T.IDN[:], T.ONES[:], [[-1, 128]], AluOpType.is_equal, 0.0, 0, 1).then_inc(S.idn, 1)
 
-    g.wait_ge(S.ld_x, 32)
-    own = X[:, ob:ob + BL]
-    tr = []
-    if is_lo:
-        tr.append(RemoteDMATransfer(dst_ids=[did(sib)], dma_engine_mask=hi, remote_sem=S.sibx,
-                                    srcs=[own], dsts=[X[:, 0:BL]]))
-        sent += n_hi
-    tr.append(RemoteDMATransfer(dst_ids=[did(lo[j]) for j in same[ci]], dma_engine_mask=off,
-                                remote_sem=S["xc%d" % ci], srcs=[own],
-                                dsts=[X[:, slot(j, ci) + ob:slot(j, ci) + ob + BL] for j in same[ci]]))
-    sent += n_off
-    g.remote_dma_fused(tr, local_sem=S.sent)
+    if is_rank:
+        sib = port[ci] if is_lo else lo[ci]
+        ob = 0 if is_lo else BL
+        xc, dc = (TK, 0) if is_lo else (BL, BL + TK)
+        wc = 0 if is_lo else 256
+        sy.dma_start(X[:, xc:xc + TK], T.x[:]).then_inc(S.ld_x, 16)
+        se.dma_start(X[:, dc:dc + TK], T.dy[:]).then_inc(S.ld_x, 16)
+        sy.dma_start(WB[:, wc:wc + 128], T.w1[:]).then_inc(S.ld_w, 16)
+        se.dma_start(WB[:, wc + 128:wc + 256], T.w2t[:]).then_inc(S.ld_w, 16)
 
-    g.wait_ge(S.ld_w, 32)
-    rid, pid = topo.addr(sib, core)
-    g.remote_dma(WB[:, wc:wc + 256], WB[:, wc:wc + 256], S.wsib, S.sent, pid, rid, hi)
-    sent += n_hi
+        g.wait_ge(S.ld_x, 32)
+        own = X[:, ob:ob + BL]
+        on = hs + [sib] if is_lo else hs
+        if on:
+            g.remote_dma_fused([RemoteDMATransfer(dst_ids=[did(d) for d in on], dma_engine_mask=hi, remote_sem=S.sibx,
+                                                  srcs=[own], dsts=[own for d in on])], local_sem=S.sent)
+            sent += n_hi
+        g.remote_dma_fused([RemoteDMATransfer(dst_ids=[did(lo[j]) for j in same[ci]], dma_engine_mask=off,
+                                              remote_sem=S["xc%d" % ci], srcs=[own],
+                                              dsts=[X[:, slot(lo[j], ci) + ob:slot(lo[j], ci) + ob + BL]
+                                                    for j in same[ci]])], local_sem=S.sent)
+        sent += n_off
+        g.wait_ge(S.ld_w, 32)
+        wd = hs + [sib]
+        g.remote_dma_fused([RemoteDMATransfer(dst_ids=[did(d) for d in wd], dma_engine_mask=wm, remote_sem=S.wsib,
+                                              srcs=[WB[:, wc:wc + 256]], dsts=[WB[:, wc:wc + 256] for d in wd])],
+                           local_sem=S.sent)
+        sent += n_wm
 
     if not is_lo:
-        g.wait_ge(S.sibx, n_hi)
-        g.remote_dma_fused([RemoteDMATransfer(dst_ids=[did(port[j]) for j in cross[ci]], dma_engine_mask=off,
+        g.wait_ge(S.sibx, n_hi if is_rank else 2 * n_hi)
+        dl = P["sendl"][core]
+        g.remote_dma_fused([RemoteDMATransfer(dst_ids=[did(rel[(j, ci)]) for j in dl], dma_engine_mask=off,
                                               remote_sem=S["xc%d" % ci], srcs=[X[:, 0:PR]],
-                                              dsts=[X[:, slot(j, ci):slot(j, ci) + PR] for j in cross[ci]])],
-                           local_sem=S.sent)
+                                              dsts=[X[:, slot(rel[(j, ci)], ci):slot(rel[(j, ci)], ci) + PR]
+                                                    for j in dl])], local_sem=S.sent)
         sent += n_off
 
-    sc = 256 - wc
+    c0 = wc if is_rank else 0
+    c1 = 256 - c0
     pe.wait_ge(S.idn, 1)
-    pe.wait_ge(S.ld_w, 32)
-    pe.transpose(T.PT0[:, 0:128], WB[:, wc:wc + 128], T.IDN[:]).then_inc(S.tp0, 1)
-    pe.wait_ge(S.wsib, n_hi)
-    pe.transpose(T.PT1[:, 0:128], WB[:, sc:sc + 128], T.IDN[:]).then_inc(S.tp1, 1)
+    if is_rank:
+        pe.wait_ge(S.ld_w, 32)
+    else:
+        pe.wait_ge(S.wsib, 2 * n_wm)
+    pe.transpose(T.PT0[:, 0:128], WB[:, c0:c0 + 128], T.IDN[:]).then_inc(S.tp0, 1)
+    if is_rank:
+        pe.wait_ge(S.wsib, n_wm)
+    pe.transpose(T.PT1[:, 0:128], WB[:, c1:c1 + 128], T.IDN[:]).then_inc(S.tp1, 1)
     se.wait_ge(S.tp0, 1)
-    se.activation(W1T[:, wc // 2:wc // 2 + 128], T.PT0[:, 0:128], ActivationFunctionType.Copy).then_inc(S.tc0, 1)
+    se.activation(W1T[:, c0 // 2:c0 // 2 + 128], T.PT0[:, 0:128], ActivationFunctionType.Copy).then_inc(S.tc0, 1)
     se.wait_ge(S.tp1, 1)
-    se.activation(W1T[:, sc // 2:sc // 2 + 128], T.PT1[:, 0:128], ActivationFunctionType.Copy).then_inc(S.tc1, 1)
+    se.activation(W1T[:, c1 // 2:c1 // 2 + 128], T.PT1[:, 0:128], ActivationFunctionType.Copy).then_inc(S.tc1, 1)
 
     cnt = {"sa": 0, "sb": 0, "vm": 0}
     halves = (_mk(_bits(off)[:n_off // 2]), _mk(_bits(off)[n_off // 2:]))
-    for k in range(1 + len(mine)):
-        if k == 0:
-            n = TK
-            xs = [(xc, TK)]
-            ds = [dc]
+    todo = ([None] if is_rank else []) + mine
+    for k, i in enumerate(todo):
+        if i is None:
+            n, x0, ds = TK, xc, [dc]
             pe.wait_ge(S.ld_x, 32)
         else:
-            i = mine[k - 1]
-            b = PR * k
-            n = BL
-            xs = [(b + TK, BL)]
-            ds = [b, b + BL + TK]
+            b = slot(core, i)
+            n, x0, ds = BL, b + TK, [b, b + BL + TK]
             pe.wait_ge(S["xc%d" % i], 2 * n_off if is_lo else n_off)
         for sh, (bank, sem) in enumerate(((T.PA, "sa"), (T.PB, "sb"))):
             w = 256 * sh
-            pe.matmul(bank[:, 0:n], WB[:, w:w + 128], X[:, xs[0][0]:xs[0][0] + xs[0][1]], True, True).then_inc(S[sem], 1)
+            pe.matmul(bank[:, 0:n], WB[:, w:w + 128], X[:, x0:x0 + n], True, True).then_inc(S[sem], 1)
             cnt[sem] += 1
             for q, d in enumerate(ds):
                 pe.matmul(bank[:, n + TK * q:n + TK * (q + 1)], WB[:, w + 128:w + 256], X[:, d:d + TK],
@@ -186,12 +213,11 @@ def rank_program(g, core, T, topo):
         pe.wait_ge(S.gb, k + 1)
         pe.matmul(T.PP[:, 0:n], W1T[:, 128:256], G[:, PR * k + BL:PR * k + BL + n], False, True).then_inc(S.pp, 1)
         ve.wait_ge(S.pp, k + 1)
-        if k == 0:
+        if i is None:
             ve.tensor_copy(R[:, 0:TK], T.PP[:, 0:n]).then_inc(S.pc, 1)
             continue
-        po = BL * (k - 1)
+        po = BL * k
         ve.tensor_copy(PO[:, po:po + BL], T.PP[:, 0:n]).then_inc(S.pc, 1)
-        i = mine[k - 1]
         rs = 1 + (same[i] + cross[i]).index(ci)
         g.wait_ge(S.pc, k + 1)
         g.remote_dma_fused([RemoteDMATransfer(dst_ids=[did(d)], dma_engine_mask=halves[t], remote_sem=S["r%d" % rs],
@@ -200,15 +226,17 @@ def rank_program(g, core, T, topo):
                             for t, d in enumerate((lo[i], port[i]))], local_sem=S.sent)
         sent += n_off
 
-    pe.wait_ge(S.pc, 1 + len(mine))
-    pe.matmul(T.PF[:, 0:TK], T.IDN[:], R[:, 0:TK], True, False)
-    for q in range(1, 1 + len(rorder)):
-        pe.wait_ge(S["r%d" % q], n_off // 2)
-        mm = pe.matmul(T.PF[:, 0:TK], T.IDN[:], R[:, TK * q:TK * (q + 1)], False, q == len(rorder))
-    mm.then_inc(S.fin, 1)
-    ve.wait_ge(S.fin, 1)
-    ve.tensor_copy(T.OUT[:], T.PF[:, 0:TK]).then_inc(S.oc, 1)
-    sy.wait_ge(S.oc, 1)
-    sy.dma_start(T.dx[:], T.OUT[:]).then_inc(S.st, 16)
-    sy.wait_ge(S.st, 16)
+    if is_rank:
+        nr = len(same[ci]) + len(cross[ci])
+        pe.wait_ge(S.pc, len(todo))
+        mm = pe.matmul(T.PF[:, 0:TK], T.IDN[:], R[:, 0:TK], True, False)
+        for q in range(1, 1 + nr):
+            pe.wait_ge(S["r%d" % q], n_off // 2)
+            mm = pe.matmul(T.PF[:, 0:TK], T.IDN[:], R[:, TK * q:TK * (q + 1)], False, q == nr)
+        mm.then_inc(S.fin, 1)
+        ve.wait_ge(S.fin, 1)
+        ve.tensor_copy(T.OUT[:], T.PF[:, 0:TK]).then_inc(S.oc, 1)
+        sy.wait_ge(S.oc, 1)
+        sy.dma_start(T.dx[:], T.OUT[:]).then_inc(S.st, 16)
+        sy.wait_ge(S.st, 16)
     g.wait_ge(S.sent, sent)

@@ -9,7 +9,7 @@ MAXG = 3
 KEEP = 2
 
 SCRATCH = {
-    "X": ("sbuf", [128, PR * (1 + MAXG)], "bfloat16"),
+    "X": ("sbuf", [128, 4 * (1 + MAXG), TK], "bfloat16"),
     "WB": ("sbuf", [128, 512], "bfloat16"),
     "W1T": ("sbuf", [128, 256], "bfloat16"),
     "ONES": ("sbuf", [128, 128], "bfloat16"),
@@ -19,15 +19,17 @@ SCRATCH = {
     "PO": ("sbuf", [128, BL * (1 + MAXG)], "bfloat16"),
     "R": ("sbuf", [128, TK * 6], "bfloat16"),
     "OUT": ("sbuf", [128, TK], "bfloat16"),
-    "PA": ("psum", [128, 512], "float32"),
-    "PB": ("psum", [128, 512], "float32"),
+    "ZA": ("psum", [128, 512], "float32"),
+    "ZB": ("psum", [128, 512], "float32"),
+    "UA": ("psum", [128, 512], "float32"),
+    "UB": ("psum", [128, 512], "float32"),
     "PP": ("psum", [128, 512], "float32"),
     "PF": ("psum", [128, 512], "float32"),
     "PT0": ("psum", [128, 1024], "bfloat16"),
     "PT1": ("psum", [128, 1024], "bfloat16"),
 }
 SEMAPHORES = (["ld_x", "ld_w", "ones", "idn", "sent", "sibx", "wsib", "tp0", "tp1", "tc0", "tc1",
-               "sa", "sb", "vm", "ga", "gb", "pp", "pc", "fin", "oc", "st"]
+               "za", "zb", "ua", "ub", "vm", "ga", "gb", "pp", "pc", "fin", "oc", "st"]
               + ["xc%d" % i for i in range(6)] + ["r%d" % i for i in range(1, 6)])
 
 
@@ -73,6 +75,8 @@ def _plan(T, topo):
     for i in range(n):
         for q, j in enumerate(cross[i]):
             rel[(i, j)] = port[i] if q < KEEP or q - KEEP >= len(helpers[i]) else helpers[i][q - KEEP]
+        for j in same[i]:
+            rel[(i, j)] = lo[i]
     role, sendl, groups = {}, {}, {}
     for i in range(n):
         role[lo[i]] = (i, "lo")
@@ -82,11 +86,10 @@ def _plan(T, topo):
     for c, (i, kind) in role.items():
         sendl[c] = sorted([j for j in cross[i] if rel[(i, j)] == c], key=lambda j: rel[(j, i)] != port[j])
     for c, (j, kind) in role.items():
-        if kind == "lo":
-            groups[c] = sorted([i for i in range(n) if j in same[i]], key=lambda i: (same[i].index(j), i))
-        else:
-            groups[c] = sorted([i for i in cross[j] if rel[(j, i)] == c],
-                               key=lambda i: (rel[(i, j)] != port[i], sendl[rel[(i, j)]].index(j), i))
+        ea = sorted([i for i in same[j] if rel[(j, i)] == c], key=lambda i: (same[i].index(j), i))
+        la = sorted([i for i in cross[j] if rel[(j, i)] == c],
+                    key=lambda i: (rel[(i, j)] != port[i], sendl[rel[(i, j)]].index(j), i))
+        groups[c] = ea + la
     return {"lo": lo, "port": port, "same": same, "cross": cross, "helpers": helpers, "rel": rel, "role": role,
             "sendl": sendl, "groups": groups}
 
@@ -108,15 +111,15 @@ def rank_program(g, core, T, topo):
         rid, pid = topo.addr(d, core)
         return DstId(rid=rid, pnc=pid)
 
-    def slot(w, i):
-        return PR * (1 + P["groups"][w].index(i))
+    def slot(j):
+        return 4 * (1 + P["groups"][rel[(j, ci)]].index(ci))
 
     far = lo[same[ci][0]] if is_rank else port[P["sendl"][core][0]]
     off = topo.mask(core, far)
     full = topo.mask(lo[ci], port[ci])
     hi = full & ~off
-    wm = full if hs else hi
-    n_off, n_hi, n_wm = len(_bits(off)), len(_bits(hi)), len(_bits(wm))
+    om = full if hs else hi
+    n_off, n_om = len(_bits(off)), len(_bits(om))
     sent = 0
 
     ve.memset(T.ONES[:], 1.0).then_inc(S.ones, 1)
@@ -125,40 +128,40 @@ def rank_program(g, core, T, topo):
 
     if is_rank:
         sib = port[ci] if is_lo else lo[ci]
-        ob = 0 if is_lo else BL
-        xc, dc = (TK, 0) if is_lo else (BL, BL + TK)
+        ob = 0 if is_lo else 2
+        xb, db = (1, 0) if is_lo else (2, 3)
         wc = 0 if is_lo else 256
-        sy.dma_start(X[:, xc:xc + TK], T.x[:]).then_inc(S.ld_x, 16)
-        se.dma_start(X[:, dc:dc + TK], T.dy[:]).then_inc(S.ld_x, 16)
+        sy.dma_start(X[:, xb, :], T.x[:]).then_inc(S.ld_x, 16)
+        se.dma_start(X[:, db, :], T.dy[:]).then_inc(S.ld_x, 16)
         sy.dma_start(WB[:, wc:wc + 128], T.w1[:]).then_inc(S.ld_w, 16)
         se.dma_start(WB[:, wc + 128:wc + 256], T.w2t[:]).then_inc(S.ld_w, 16)
 
         g.wait_ge(S.ld_x, 32)
-        own = X[:, ob:ob + BL]
+        own = X[:, ob:ob + 2, :]
         on = hs + [sib] if is_lo else hs
         if on:
-            g.remote_dma_fused([RemoteDMATransfer(dst_ids=[did(d) for d in on], dma_engine_mask=hi, remote_sem=S.sibx,
-                                                  srcs=[own], dsts=[own for d in on])], local_sem=S.sent)
-            sent += n_hi
-        g.remote_dma_fused([RemoteDMATransfer(dst_ids=[did(lo[j]) for j in same[ci]], dma_engine_mask=off,
+            g.remote_dma_fused([RemoteDMATransfer(dst_ids=[did(d) for d in on], dma_engine_mask=om,
+                                                  remote_sem=S.sibx, srcs=[own], dsts=[own for d in on])],
+                               local_sem=S.sent)
+            sent += n_om
+        g.remote_dma_fused([RemoteDMATransfer(dst_ids=[did(rel[(j, ci)]) for j in same[ci]], dma_engine_mask=off,
                                               remote_sem=S["xc%d" % ci], srcs=[own],
-                                              dsts=[X[:, slot(lo[j], ci) + ob:slot(lo[j], ci) + ob + BL]
-                                                    for j in same[ci]])], local_sem=S.sent)
+                                              dsts=[X[:, slot(j) + ob:slot(j) + ob + 2, :] for j in same[ci]])],
+                           local_sem=S.sent)
         sent += n_off
         g.wait_ge(S.ld_w, 32)
         wd = hs + [sib]
-        g.remote_dma_fused([RemoteDMATransfer(dst_ids=[did(d) for d in wd], dma_engine_mask=wm, remote_sem=S.wsib,
+        g.remote_dma_fused([RemoteDMATransfer(dst_ids=[did(d) for d in wd], dma_engine_mask=om, remote_sem=S.wsib,
                                               srcs=[WB[:, wc:wc + 256]], dsts=[WB[:, wc:wc + 256] for d in wd])],
                            local_sem=S.sent)
-        sent += n_wm
+        sent += n_om
 
     if not is_lo:
-        g.wait_ge(S.sibx, n_hi if is_rank else 2 * n_hi)
+        g.wait_ge(S.sibx, n_om if is_rank else 2 * n_om)
         dl = P["sendl"][core]
         g.remote_dma_fused([RemoteDMATransfer(dst_ids=[did(rel[(j, ci)]) for j in dl], dma_engine_mask=off,
-                                              remote_sem=S["xc%d" % ci], srcs=[X[:, 0:PR]],
-                                              dsts=[X[:, slot(rel[(j, ci)], ci):slot(rel[(j, ci)], ci) + PR]
-                                                    for j in dl])], local_sem=S.sent)
+                                              remote_sem=S["xc%d" % ci], srcs=[X[:, 0:4, :]],
+                                              dsts=[X[:, slot(j):slot(j) + 4, :] for j in dl])], local_sem=S.sent)
         sent += n_off
 
     c0 = wc if is_rank else 0
@@ -167,51 +170,49 @@ def rank_program(g, core, T, topo):
     if is_rank:
         pe.wait_ge(S.ld_w, 32)
     else:
-        pe.wait_ge(S.wsib, 2 * n_wm)
+        pe.wait_ge(S.wsib, 2 * n_om)
     pe.transpose(T.PT0[:, 0:128], WB[:, c0:c0 + 128], T.IDN[:]).then_inc(S.tp0, 1)
     if is_rank:
-        pe.wait_ge(S.wsib, n_wm)
+        pe.wait_ge(S.wsib, n_om)
     pe.transpose(T.PT1[:, 0:128], WB[:, c1:c1 + 128], T.IDN[:]).then_inc(S.tp1, 1)
     se.wait_ge(S.tp0, 1)
     se.activation(W1T[:, c0 // 2:c0 // 2 + 128], T.PT0[:, 0:128], ActivationFunctionType.Copy).then_inc(S.tc0, 1)
     se.wait_ge(S.tp1, 1)
     se.activation(W1T[:, c1 // 2:c1 // 2 + 128], T.PT1[:, 0:128], ActivationFunctionType.Copy).then_inc(S.tc1, 1)
 
-    cnt = {"sa": 0, "sb": 0, "vm": 0}
     halves = (_mk(_bits(off)[:n_off // 2]), _mk(_bits(off)[n_off // 2:]))
-    todo = ([None] if is_rank else []) + mine
+    todo = mine + ([None] if is_rank else [])
     for k, i in enumerate(todo):
         if i is None:
-            n, x0, ds = TK, xc, [dc]
+            n, xs, ds = TK, X[:, xb, :], X[:, db, :]
             pe.wait_ge(S.ld_x, 32)
         else:
-            b = slot(core, i)
-            n, x0, ds = BL, b + TK, [b, b + BL + TK]
-            pe.wait_ge(S["xc%d" % i], 2 * n_off if is_lo else n_off)
-        for sh, (bank, sem) in enumerate(((T.PA, "sa"), (T.PB, "sb"))):
-            w = 256 * sh
-            pe.matmul(bank[:, 0:n], WB[:, w:w + 128], X[:, x0:x0 + n], True, True).then_inc(S[sem], 1)
-            cnt[sem] += 1
-            for q, d in enumerate(ds):
-                pe.matmul(bank[:, n + TK * q:n + TK * (q + 1)], WB[:, w + 128:w + 256], X[:, d:d + TK],
-                          True, True).then_inc(S[sem], 1)
-                cnt[sem] += 1
-        for sh, (bank, sem, gs) in enumerate(((T.PA, "sa", S.ga), (T.PB, "sb", S.gb))):
-            c = PR * k + BL * sh
-            ve.wait_ge(S[sem], cnt[sem])
-            ve.tensor_scalar(M[:, c:c + n], bank[:, 0:n], 0.0, None, AluOpType.is_gt).then_inc(S.vm, 1)
-            cnt["vm"] += 1
-            ve.wait_ge(S.vm, cnt["vm"])
-            ve.tensor_tensor(G[:, c:c + n], M[:, c:c + n], bank[:, n:2 * n], AluOpType.mult).then_inc(gs, 1)
+            b = 4 * (1 + mine.index(i))
+            n, xs, ds = BL, X[:, b + 1:b + 3, :], X[:, b:b + 4:3, :]
+            pe.wait_ge(S["xc%d" % i], 2 * n_off if i in same[ci] else n_off)
+        ca, cb = PR * k, PR * k + BL
+        pe.matmul(T.ZA[:, 0:n], WB[:, 0:128], xs, True, True).then_inc(S.za, 1)
+        pe.matmul(T.ZB[:, 0:n], WB[:, 256:384], xs, True, True).then_inc(S.zb, 1)
+        pe.matmul(T.UA[:, 0:n], WB[:, 128:256], ds, True, True).then_inc(S.ua, 1)
+        pe.matmul(T.UB[:, 0:n], WB[:, 384:512], ds, True, True).then_inc(S.ub, 1)
+        ve.wait_ge(S.za, k + 1)
+        ve.tensor_scalar(M[:, ca:ca + n], T.ZA[:, 0:n], 0.0, None, AluOpType.is_gt).then_inc(S.vm, 1)
+        ve.wait_ge(S.zb, k + 1)
+        ve.tensor_scalar(M[:, cb:cb + n], T.ZB[:, 0:n], 0.0, None, AluOpType.is_gt).then_inc(S.vm, 1)
+        ve.wait_ge(S.vm, 2 * (k + 1))
+        ve.wait_ge(S.ua, k + 1)
+        ve.tensor_tensor(G[:, ca:ca + n], M[:, ca:ca + n], T.UA[:, 0:n], AluOpType.mult).then_inc(S.ga, 1)
+        ve.wait_ge(S.ub, k + 1)
+        ve.tensor_tensor(G[:, cb:cb + n], M[:, cb:cb + n], T.UB[:, 0:n], AluOpType.mult).then_inc(S.gb, 1)
         if k == 0:
             pe.wait_ge(S.tc0, 1)
             pe.wait_ge(S.tc1, 1)
         else:
             pe.wait_ge(S.pc, k)
         pe.wait_ge(S.ga, k + 1)
-        pe.matmul(T.PP[:, 0:n], W1T[:, 0:128], G[:, PR * k:PR * k + n], True, False)
+        pe.matmul(T.PP[:, 0:n], W1T[:, 0:128], G[:, ca:ca + n], True, False)
         pe.wait_ge(S.gb, k + 1)
-        pe.matmul(T.PP[:, 0:n], W1T[:, 128:256], G[:, PR * k + BL:PR * k + BL + n], False, True).then_inc(S.pp, 1)
+        pe.matmul(T.PP[:, 0:n], W1T[:, 128:256], G[:, cb:cb + n], False, True).then_inc(S.pp, 1)
         ve.wait_ge(S.pp, k + 1)
         if i is None:
             ve.tensor_copy(R[:, 0:TK], T.PP[:, 0:n]).then_inc(S.pc, 1)

@@ -7,6 +7,7 @@ BL = 2 * TK
 PR = 2 * BL
 MAXG = 3
 KEEP = 2
+LOG = 2
 
 SCRATCH = {
     "X": ("sbuf", [128, 4 * (1 + MAXG), TK], "bfloat16"),
@@ -28,7 +29,7 @@ SCRATCH = {
     "PT0": ("psum", [128, 1024], "bfloat16"),
     "PT1": ("psum", [128, 1024], "bfloat16"),
 }
-SEMAPHORES = (["ld_x", "ld_w", "ones", "idn", "sent", "sibx", "wsib", "tp0", "tp1", "tc0", "tc1",
+SEMAPHORES = (["ld_x", "ld_w", "ones", "idn", "idx", "sent", "sibx", "wsib", "tp0", "tp1", "tc0", "tc1",
                "za", "zb", "ua", "ub", "vm", "ga", "gb", "pp", "pc", "fin", "oc", "st"]
               + ["xc%d" % i for i in range(6)] + ["r%d" % i for i in range(1, 6)])
 
@@ -63,35 +64,44 @@ def _plan(T, topo):
         p = [c for c in mem[k] if owner(c)][-1]
         port.append(p)
         lo.append([c for c in mem[k] if c != p][0])
-    same, cross, helpers = [], [], []
+    same, cross, relays, xserve, sserve = [], [], [], [], []
     for i in range(n):
         peers = sorted([j for j in range(n) if j != i], key=lambda j: (j - i) % n)
         same.append([j for j in peers if topo.may_write(lo[i], lo[j])])
         cross.append([j for j in peers if not topo.may_write(lo[i], lo[j])])
-        idle = [c for c in range(NSIM) if (topo.host(c), topo.chip(c)) == keys[i] and c not in cores and owner(c)]
-        idle.sort(key=lambda c: (topo.die(c) != topo.die(port[i]), c))
-        helpers.append(idle[:max(0, len(cross[i]) - KEEP)])
-    rel = {}
+        idle = [c for c in range(NSIM) if (topo.host(c), topo.chip(c)) == keys[i] and c not in cores]
+        own = sorted([c for c in idle if owner(c)], key=lambda c: (topo.die(c) != topo.die(port[i]), c))
+        oth = sorted([c for c in idle if not owner(c) and topo.die(c) == topo.die(lo[i])])
+        nrel = max(0, len(cross[i]) - KEEP)
+        relays.append(own[:nrel])
+        xserve.append(own[nrel:nrel + KEEP - 1])
+        sserve.append(oth[:max(0, len(same[i]) - LOG)])
+    snd, rel = {}, {}
     for i in range(n):
         for q, j in enumerate(cross[i]):
-            rel[(i, j)] = port[i] if q < KEEP or q - KEEP >= len(helpers[i]) else helpers[i][q - KEEP]
-        for j in same[i]:
-            rel[(i, j)] = lo[i]
+            snd[(i, j)] = port[i] if q < KEEP or q - KEEP >= len(relays[i]) else relays[i][q - KEEP]
+            if q == 0 or snd[(i, j)] != port[i]:
+                rel[(i, j)] = snd[(i, j)]
+            else:
+                rel[(i, j)] = xserve[i][q - 1] if q - 1 < len(xserve[i]) else port[i]
+        ea = sorted(same[i], key=lambda j: (same[j].index(i), j))
+        for q, j in enumerate(ea):
+            rel[(i, j)] = lo[i] if q < LOG or q - LOG >= len(sserve[i]) else sserve[i][q - LOG]
     role, sendl, groups = {}, {}, {}
     for i in range(n):
         role[lo[i]] = (i, "lo")
         role[port[i]] = (i, "port")
-        for h in helpers[i]:
+        for h in relays[i] + xserve[i] + sserve[i]:
             role[h] = (i, "helper")
     for c, (i, kind) in role.items():
-        sendl[c] = sorted([j for j in cross[i] if rel[(i, j)] == c], key=lambda j: rel[(j, i)] != port[j])
+        sendl[c] = sorted([j for j in cross[i] if snd[(i, j)] == c], key=lambda j: rel[(j, i)] != port[j])
     for c, (j, kind) in role.items():
         ea = sorted([i for i in same[j] if rel[(j, i)] == c], key=lambda i: (same[i].index(j), i))
         la = sorted([i for i in cross[j] if rel[(j, i)] == c],
-                    key=lambda i: (rel[(i, j)] != port[i], sendl[rel[(i, j)]].index(j), i))
+                    key=lambda i: (snd[(i, j)] != port[i], sendl[snd[(i, j)]].index(j), i))
         groups[c] = ea + la
-    return {"lo": lo, "port": port, "same": same, "cross": cross, "helpers": helpers, "rel": rel, "role": role,
-            "sendl": sendl, "groups": groups}
+    return {"lo": lo, "port": port, "same": same, "cross": cross, "relays": relays, "xserve": xserve, "sserve": sserve,
+            "rel": rel, "role": role, "sendl": sendl, "groups": groups}
 
 
 def rank_program(g, core, T, topo):
@@ -101,7 +111,8 @@ def rank_program(g, core, T, topo):
     S = T.sem
     ci, kind = P["role"][core]
     lo, port, same, cross, rel = P["lo"], P["port"], P["same"], P["cross"], P["rel"]
-    hs = P["helpers"][ci]
+    hs = P["relays"][ci]
+    allh = hs + P["xserve"][ci] + P["sserve"][ci]
     mine = P["groups"][core]
     is_lo, is_rank = kind == "lo", kind != "helper"
     X, WB, W1T, M, G, PO, R = T.X, T.WB, T.W1T, T.M, T.G, T.PO, T.R
@@ -114,7 +125,7 @@ def rank_program(g, core, T, topo):
     def slot(j):
         return 4 * (1 + P["groups"][rel[(j, ci)]].index(ci))
 
-    far = lo[same[ci][0]] if is_rank else port[P["sendl"][core][0]]
+    far = lo[same[ci][0]] if is_rank else lo[mine[0]]
     off = topo.mask(core, far)
     full = topo.mask(lo[ci], port[ci])
     hi = full & ~off
@@ -122,9 +133,22 @@ def rank_program(g, core, T, topo):
     n_off, n_om = len(_bits(off)), len(_bits(om))
     sent = 0
 
+    team = [lo[ci], port[ci]] if is_rank else allh
+    m = len(team)
+    wid = (128 // m) // 16 * 16
+    a = wid * team.index(core)
+    b = a + wid if team.index(core) < m - 1 else 128
+    im = full if is_rank else off
     ve.memset(T.ONES[:], 1.0).then_inc(S.ones, 1)
     g.wait_ge(S.ones, 1)
-    g.affine_select(T.IDN[:], T.ONES[:], [[-1, 128]], AluOpType.is_equal, 0.0, 0, 1).then_inc(S.idn, 1)
+    g.affine_select(T.IDN[:, a:b], T.ONES[:, a:b], [[-1, b - a]], AluOpType.is_equal, 0.0, -a, 1).then_inc(S.idn, 1)
+    others = [d for d in team if d != core]
+    if others:
+        g.wait_ge(S.idn, 1)
+        g.remote_dma_fused([RemoteDMATransfer(dst_ids=[did(d) for d in others], dma_engine_mask=im, remote_sem=S.idx,
+                                              srcs=[T.IDN[:, a:b]], dsts=[T.IDN[:, a:b] for d in others])],
+                           local_sem=S.sent)
+        sent += len(_bits(im))
 
     if is_rank:
         sib = port[ci] if is_lo else lo[ci]
@@ -138,7 +162,7 @@ def rank_program(g, core, T, topo):
 
         g.wait_ge(S.ld_x, 32)
         own = X[:, ob:ob + 2, :]
-        on = hs + [sib] if is_lo else hs
+        on = [sib] + hs if is_lo else hs
         if on:
             g.remote_dma_fused([RemoteDMATransfer(dst_ids=[did(d) for d in on], dma_engine_mask=om,
                                                   remote_sem=S.sibx, srcs=[own], dsts=[own for d in on])],
@@ -150,15 +174,16 @@ def rank_program(g, core, T, topo):
                            local_sem=S.sent)
         sent += n_off
         g.wait_ge(S.ld_w, 32)
-        wd = hs + [sib]
-        g.remote_dma_fused([RemoteDMATransfer(dst_ids=[did(d) for d in wd], dma_engine_mask=om, remote_sem=S.wsib,
-                                              srcs=[WB[:, wc:wc + 256]], dsts=[WB[:, wc:wc + 256] for d in wd])],
-                           local_sem=S.sent)
-        sent += n_om
+        for wd in ([sib], allh):
+            if wd:
+                g.remote_dma_fused([RemoteDMATransfer(dst_ids=[did(d) for d in wd], dma_engine_mask=om,
+                                                      remote_sem=S.wsib, srcs=[WB[:, wc:wc + 256]],
+                                                      dsts=[WB[:, wc:wc + 256] for d in wd])], local_sem=S.sent)
+                sent += n_om
 
-    if not is_lo:
+    dl = P["sendl"][core]
+    if dl:
         g.wait_ge(S.sibx, n_om if is_rank else 2 * n_om)
-        dl = P["sendl"][core]
         g.remote_dma_fused([RemoteDMATransfer(dst_ids=[did(rel[(j, ci)]) for j in dl], dma_engine_mask=off,
                                               remote_sem=S["xc%d" % ci], srcs=[X[:, 0:4, :]],
                                               dsts=[X[:, slot(j):slot(j) + 4, :] for j in dl])], local_sem=S.sent)
@@ -167,6 +192,8 @@ def rank_program(g, core, T, topo):
     c0 = wc if is_rank else 0
     c1 = 256 - c0
     pe.wait_ge(S.idn, 1)
+    if others:
+        pe.wait_ge(S.idx, len(_bits(im)) * len(others))
     if is_rank:
         pe.wait_ge(S.ld_w, 32)
     else:
@@ -231,12 +258,13 @@ def rank_program(g, core, T, topo):
         nr = len(same[ci]) + len(cross[ci])
         pe.wait_ge(S.pc, len(todo))
         mm = pe.matmul(T.PF[:, 0:TK], T.IDN[:], R[:, 0:TK], True, False)
-        for q in range(1, 1 + nr):
+        for q in range(1, nr):
             pe.wait_ge(S["r%d" % q], n_off // 2)
-            mm = pe.matmul(T.PF[:, 0:TK], T.IDN[:], R[:, TK * q:TK * (q + 1)], False, q == nr)
+            mm = pe.matmul(T.PF[:, 0:TK], T.IDN[:], R[:, TK * q:TK * (q + 1)], False, q == nr - 1)
         mm.then_inc(S.fin, 1)
         ve.wait_ge(S.fin, 1)
-        ve.tensor_copy(T.OUT[:], T.PF[:, 0:TK]).then_inc(S.oc, 1)
+        ve.wait_ge(S["r%d" % nr], n_off // 2)
+        ve.tensor_tensor(T.OUT[:], R[:, TK * nr:TK * (nr + 1)], T.PF[:, 0:TK], AluOpType.add).then_inc(S.oc, 1)
         sy.wait_ge(S.oc, 1)
         sy.dma_start(T.dx[:], T.OUT[:]).then_inc(S.st, 16)
         sy.wait_ge(S.st, 16)

from concourse.bass import DstId, RemoteDMATransfer
from concourse.mybir import AluOpType, ActivationFunctionType

NSIM = 256
TK = 32
BL = 2 * TK
PR = 2 * BL
MAXG = 3
KEEP = 2
LOG = 2

SCRATCH = {
    "X": ("sbuf", [128, 4 * (1 + MAXG), TK], "bfloat16"),
    "WB": ("sbuf", [128, 512], "bfloat16"),
    "W1T": ("sbuf", [128, 256], "bfloat16"),
    "ONES": ("sbuf", [128, 128], "bfloat16"),
    "IDN": ("sbuf", [128, 128], "bfloat16"),
    "M": ("sbuf", [128, PR * (1 + MAXG)], "bfloat16"),
    "G": ("sbuf", [128, PR * (1 + MAXG)], "bfloat16"),
    "PO": ("sbuf", [128, BL * (1 + MAXG)], "bfloat16"),
    "R": ("sbuf", [128, TK * 6], "bfloat16"),
    "OUT": ("sbuf", [128, TK], "bfloat16"),
    "ZA": ("psum", [128, 512], "float32"),
    "ZB": ("psum", [128, 512], "float32"),
    "UA": ("psum", [128, 512], "float32"),
    "UB": ("psum", [128, 512], "float32"),
    "PP": ("psum", [128, 512], "float32"),
    "PF": ("psum", [128, 512], "float32"),
    "PT0": ("psum", [128, 1024], "bfloat16"),
    "PT1": ("psum", [128, 1024], "bfloat16"),
}
SEMAPHORES = (["ld_x", "ld_w", "ones", "idn", "idx", "sent", "sibx", "wsib", "tp0", "tp1", "tc0", "tc1",
               "za", "zb", "ua", "ub", "vm", "ga", "gb", "pp", "pc", "fin", "oc", "st"]
              + ["xc%d" % i for i in range(6)] + ["r%d" % i for i in range(1, 6)])


def _bits(mask):
    return [i for i in range(16) if (mask >> i) & 1]


def _mk(bits):
    m = 0
    for b in bits:
        m |= 1 << b
    return m


def _plan(T, topo):
    cores = list(T.cores)
    keys, mem = [], {}
    for c in cores:
        k = (topo.host(c), topo.chip(c))
        if k not in mem:
            keys.append(k)
            mem[k] = []
        mem[k].append(c)
    n = len(keys)

    def owner(c):
        return all(topo.may_write(c, o) for o in cores if o != c)

    lo, port = [], []
    for k in keys:
        p = [c for c in mem[k] if owner(c)][-1]
        port.append(p)
        lo.append([c for c in mem[k] if c != p][0])
    same, cross, relays, xserve, sserve = [], [], [], [], []
    for i in range(n):
        peers = sorted([j for j in range(n) if j != i], key=lambda j: (j - i) % n)
        same.append([j for j in peers if topo.may_write(lo[i], lo[j])])
        cross.append([j for j in peers if not topo.may_write(lo[i], lo[j])])
        idle = [c for c in range(NSIM) if (topo.host(c), topo.chip(c)) == keys[i] and c not in cores]
        own = sorted([c for c in idle if owner(c)], key=lambda c: (topo.die(c) != topo.die(port[i]), c))
        oth = sorted([c for c in idle if not owner(c) and topo.die(c) == topo.die(lo[i])])
        nrel = max(0, len(cross[i]) - KEEP)
        relays.append(own[:nrel])
        xserve.append(own[nrel:nrel + KEEP - 1])
        sserve.append(oth[:max(0, len(same[i]) - LOG)])
    snd, rel = {}, {}
    for i in range(n):
        for q, j in enumerate(cross[i]):
            snd[(i, j)] = port[i] if q < KEEP or q - KEEP >= len(relays[i]) else relays[i][q - KEEP]
            if q == 0 or snd[(i, j)] != port[i]:
                rel[(i, j)] = snd[(i, j)]
            else:
                rel[(i, j)] = xserve[i][q - 1] if q - 1 < len(xserve[i]) else port[i]
        ea = sorted(same[i], key=lambda j: (same[j].index(i), j))
        for q, j in enumerate(ea):
            rel[(i, j)] = lo[i] if q < LOG or q - LOG >= len(sserve[i]) else sserve[i][q - LOG]
    role, sendl, groups = {}, {}, {}
    for i in range(n):
        role[lo[i]] = (i, "lo")
        role[port[i]] = (i, "port")
        for h in relays[i] + xserve[i] + sserve[i]:
            role[h] = (i, "helper")
    for c, (i, kind) in role.items():
        sendl[c] = sorted([j for j in cross[i] if snd[(i, j)] == c], key=lambda j: rel[(j, i)] != port[j])
    for c, (j, kind) in role.items():
        ea = sorted([i for i in same[j] if rel[(j, i)] == c], key=lambda i: (same[i].index(j), i))
        la = sorted([i for i in cross[j] if rel[(j, i)] == c],
                    key=lambda i: (snd[(i, j)] != port[i], sendl[snd[(i, j)]].index(j), i))
        groups[c] = ea + la
    return {"lo": lo, "port": port, "same": same, "cross": cross, "relays": relays, "xserve": xserve, "sserve": sserve,
            "rel": rel, "role": role, "sendl": sendl, "groups": groups}


def rank_program(g, core, T, topo):
    P = _plan(T, topo)
    if core not in P["role"]:
        return
    S = T.sem
    ci, kind = P["role"][core]
    lo, port, same, cross, rel = P["lo"], P["port"], P["same"], P["cross"], P["rel"]
    hs = P["relays"][ci]
    allh = hs + P["xserve"][ci] + P["sserve"][ci]
    mine = P["groups"][core]
    is_lo, is_rank = kind == "lo", kind != "helper"
    X, WB, W1T, M, G, PO, R = T.X, T.WB, T.W1T, T.M, T.G, T.PO, T.R
    pe, ve, se, sy = g.tensor, g.vector, g.scalar, g.sync

    def did(d):
        rid, pid = topo.addr(d, core)
        return DstId(rid=rid, pnc=pid)

    def slot(j):
        return 4 * (1 + P["groups"][rel[(j, ci)]].index(ci))

    far = lo[same[ci][0]] if is_rank else lo[mine[0]]
    off = topo.mask(core, far)
    full = topo.mask(lo[ci], port[ci])
    hi = full & ~off
    om = full if hs else hi
    n_off, n_om = len(_bits(off)), len(_bits(om))
    sent = 0

    team = [lo[ci], port[ci]] if is_rank else allh
    m = len(team)
    wid = (128 // m) // 16 * 16
    a = wid * team.index(core)
    b = a + wid if team.index(core) < m - 1 else 128
    im = full if is_rank else off
    ve.memset(T.ONES[:], 1.0).then_inc(S.ones, 1)
    g.wait_ge(S.ones, 1)
    g.affine_select(T.IDN[:, a:b], T.ONES[:, a:b], [[-1, b - a]], AluOpType.is_equal, 0.0, -a, 1).then_inc(S.idn, 1)
    others = [d for d in team if d != core]
    if others:
        g.wait_ge(S.idn, 1)
        g.remote_dma_fused([RemoteDMATransfer(dst_ids=[did(d) for d in others], dma_engine_mask=im, remote_sem=S.idx,
                                              srcs=[T.IDN[:, a:b]], dsts=[T.IDN[:, a:b] for d in others])],
                           local_sem=S.sent)
        sent += len(_bits(im))

    if is_rank:
        sib = port[ci] if is_lo else lo[ci]
        ob = 0 if is_lo else 2
        xb, db = (1, 0) if is_lo else (2, 3)
        wc = 0 if is_lo else 256
        sy.dma_start(X[:, xb, :], T.x[:]).then_inc(S.ld_x, 16)
        se.dma_start(X[:, db, :], T.dy[:]).then_inc(S.ld_x, 16)
        sy.dma_start(WB[:, wc:wc + 128], T.w1[:]).then_inc(S.ld_w, 16)
        se.dma_start(WB[:, wc + 128:wc + 256], T.w2t[:]).then_inc(S.ld_w, 16)

        g.wait_ge(S.ld_x, 32)
        own = X[:, ob:ob + 2, :]
        on = [sib] + hs if is_lo else hs
        if on:
            g.remote_dma_fused([RemoteDMATransfer(dst_ids=[did(d) for d in on], dma_engine_mask=om,
                                                  remote_sem=S.sibx, srcs=[own], dsts=[own for d in on])],
                               local_sem=S.sent)
            sent += n_om
        g.remote_dma_fused([RemoteDMATransfer(dst_ids=[did(rel[(j, ci)]) for j in same[ci]], dma_engine_mask=off,
                                              remote_sem=S["xc%d" % ci], srcs=[own],
                                              dsts=[X[:, slot(j) + ob:slot(j) + ob + 2, :] for j in same[ci]])],
                           local_sem=S.sent)
        sent += n_off
        g.wait_ge(S.ld_w, 32)
        for wd in ([sib], allh):
            if wd:
                g.remote_dma_fused([RemoteDMATransfer(dst_ids=[did(d) for d in wd], dma_engine_mask=om,
                                                      remote_sem=S.wsib, srcs=[WB[:, wc:wc + 256]],
                                                      dsts=[WB[:, wc:wc + 256] for d in wd])], local_sem=S.sent)
                sent += n_om

    dl = P["sendl"][core]
    if dl:
        g.wait_ge(S.sibx, n_om if is_rank else 2 * n_om)
        g.remote_dma_fused([RemoteDMATransfer(dst_ids=[did(rel[(j, ci)]) for j in dl], dma_engine_mask=off,
                                              remote_sem=S["xc%d" % ci], srcs=[X[:, 0:4, :]],
                                              dsts=[X[:, slot(j):slot(j) + 4, :] for j in dl])], local_sem=S.sent)
        sent += n_off

    c0 = wc if is_rank else 0
    c1 = 256 - c0
    pe.wait_ge(S.idn, 1)
    if others:
        pe.wait_ge(S.idx, len(_bits(im)) * len(others))
    if is_rank:
        pe.wait_ge(S.ld_w, 32)
    else:
        pe.wait_ge(S.wsib, 2 * n_om)
    pe.transpose(T.PT0[:, 0:128], WB[:, c0:c0 + 128], T.IDN[:]).then_inc(S.tp0, 1)
    if is_rank:
        pe.wait_ge(S.wsib, n_om)
    pe.transpose(T.PT1[:, 0:128], WB[:, c1:c1 + 128], T.IDN[:]).then_inc(S.tp1, 1)
    se.wait_ge(S.tp0, 1)
    se.activation(W1T[:, c0 // 2:c0 // 2 + 128], T.PT0[:, 0:128], ActivationFunctionType.Copy).then_inc(S.tc0, 1)
    se.wait_ge(S.tp1, 1)
    se.activation(W1T[:, c1 // 2:c1 // 2 + 128], T.PT1[:, 0:128], ActivationFunctionType.Copy).then_inc(S.tc1, 1)

    halves = (_mk(_bits(off)[:n_off // 2]), _mk(_bits(off)[n_off // 2:]))
    todo = mine + ([None] if is_rank else [])
    for k, i in enumerate(todo):
        if i is None:
            n, xs, ds = TK, X[:, xb, :], X[:, db, :]
            pe.wait_ge(S.ld_x, 32)
        else:
            b = 4 * (1 + mine.index(i))
            n, xs, ds = BL, X[:, b + 1:b + 3, :], X[:, b:b + 4:3, :]
            pe.wait_ge(S["xc%d" % i], 2 * n_off if i in same[ci] else n_off)
        ca, cb = PR * k, PR * k + BL
        pe.matmul(T.ZA[:, 0:n], WB[:, 0:128], xs, True, True).then_inc(S.za, 1)
        pe.matmul(T.ZB[:, 0:n], WB[:, 256:384], xs, True, True).then_inc(S.zb, 1)
        pe.matmul(T.UA[:, 0:n], WB[:, 128:256], ds, True, True).then_inc(S.ua, 1)
        pe.matmul(T.UB[:, 0:n], WB[:, 384:512], ds, True, True).then_inc(S.ub, 1)
        ve.wait_ge(S.za, k + 1)
        ve.tensor_scalar(M[:, ca:ca + n], T.ZA[:, 0:n], 0.0, None, AluOpType.is_gt).then_inc(S.vm, 1)
        ve.wait_ge(S.zb, k + 1)
        ve.tensor_scalar(M[:, cb:cb + n], T.ZB[:, 0:n], 0.0, None, AluOpType.is_gt).then_inc(S.vm, 1)
        ve.wait_ge(S.vm, 2 * (k + 1))
        ve.wait_ge(S.ua, k + 1)
        ve.tensor_tensor(G[:, ca:ca + n], M[:, ca:ca + n], T.UA[:, 0:n], AluOpType.mult).then_inc(S.ga, 1)
        ve.wait_ge(S.ub, k + 1)
        ve.tensor_tensor(G[:, cb:cb + n], M[:, cb:cb + n], T.UB[:, 0:n], AluOpType.mult).then_inc(S.gb, 1)
        if k == 0:
            pe.wait_ge(S.tc0, 1)
            pe.wait_ge(S.tc1, 1)
        else:
            pe.wait_ge(S.pc, k)
        pe.wait_ge(S.ga, k + 1)
        pe.matmul(T.PP[:, 0:n], W1T[:, 0:128], G[:, ca:ca + n], True, False)
        pe.wait_ge(S.gb, k + 1)
        pe.matmul(T.PP[:, 0:n], W1T[:, 128:256], G[:, cb:cb + n], False, True).then_inc(S.pp, 1)
        ve.wait_ge(S.pp, k + 1)
        if i is None:
            ve.tensor_copy(R[:, 0:TK], T.PP[:, 0:n]).then_inc(S.pc, 1)
            continue
        po = BL * k
        ve.tensor_copy(PO[:, po:po + BL], T.PP[:, 0:n]).then_inc(S.pc, 1)
        rs = 1 + (same[i] + cross[i]).index(ci)
        g.wait_ge(S.pc, k + 1)
        g.remote_dma_fused([RemoteDMATransfer(dst_ids=[did(d)], dma_engine_mask=halves[t], remote_sem=S["r%d" % rs],
                                              srcs=[PO[:, po + TK * t:po + TK * (t + 1)]],
                                              dsts=[R[:, TK * rs:TK * (rs + 1)]])
                            for t, d in enumerate((lo[i], port[i]))], local_sem=S.sent)
        sent += n_off

    if is_rank:
        nr = len(same[ci]) + len(cross[ci])
        pe.wait_ge(S.pc, len(todo))
        mm = pe.matmul(T.PF[:, 0:TK], T.IDN[:], R[:, 0:TK], True, False)
        for q in range(1, nr):
            pe.wait_ge(S["r%d" % q], n_off // 2)
            mm = pe.matmul(T.PF[:, 0:TK], T.IDN[:], R[:, TK * q:TK * (q + 1)], False, q == nr - 1)
        mm.then_inc(S.fin, 1)
        ve.wait_ge(S.fin, 1)
        ve.wait_ge(S["r%d" % nr], n_off // 2)
        ve.tensor_tensor(T.OUT[:], R[:, TK * nr:TK * (nr + 1)], T.PF[:, 0:TK], AluOpType.add).then_inc(S.oc, 1)
        sy.wait_ge(S.oc, 1)
        sy.dma_start(T.dx[:], T.OUT[:]).then_inc(S.st, 16)
        sy.wait_ge(S.st, 16)
    g.wait_ge(S.sent, sent)
